import numpy as np
import ml_dtypes


def mxq(x, axis, fmt="e4m3"):
    dtype, down = {"e4m3": (ml_dtypes.float8_e4m3fn, 7), "e5m2": (ml_dtypes.float8_e5m2, 14)}[fmt]
    v = np.moveaxis(np.asarray(x, np.float32).astype(ml_dtypes.bfloat16).astype(np.float64), axis, -1)
    blocks = v.reshape(v.shape[:-1] + (-1, 32))
    amax = np.abs(blocks).max(-1, keepdims=True)
    byte = np.maximum(np.where(amax > 0, np.frexp(amax)[1] - 1 + 127, 0) - down, 1)
    scale = np.exp2(byte - 127.0)
    codes = (blocks / scale).astype(np.float32).astype(dtype).astype(np.float64)
    return np.moveaxis((codes * scale).reshape(v.shape), -1, axis)


WIDE = False


def mx_kscale(k):
    if not WIDE:
        return np.ones(k)
    levels = np.array([10, -10, 5, -5, 0])
    if k % 512:
        return np.exp2(np.random.permutation(np.resize(levels, k // 32))).repeat(32)
    a = np.empty((k // 512, 16))
    for p in range(k // 512):
        a[p, :8] = np.random.permutation(np.resize(levels, 8))
        for g in range(8):
            far = levels[np.abs(levels - a[p, g]) >= 10]
            a[p, g + 8] = far[np.random.randint(len(far))]
    return np.exp2(a.ravel()).repeat(32)


def f64(x):
    return np.asarray(x).astype(np.float64)


def striped(idx):
    return np.tile(idx.reshape(-1, 16).T, (8, 1)).astype(np.uint16)


def unstriped(offs):
    return offs[:16].T.reshape(-1).astype(np.int64)


E2M1 = np.array([0.0, 0.5, 1.0, 1.5, 2.0, 3.0, 4.0, 6.0, -0.0, -0.5, -1.0, -1.5, -2.0, -3.0, -4.0, -6.0])


def pack_weight(w, fmt):
    k, n = w.shape
    w = f64(np.asarray(w, np.float32).astype(ml_dtypes.bfloat16)).reshape(k // 32, 32, n)
    amax = np.abs(w).max(1)
    if fmt == "e4m3":
        byte = np.frexp(amax)[1] - 1 + 127 - 7
    else:
        mant, ex = np.frexp(amax / 6.0)
        byte = np.where(mant > 0.5, ex, ex - 1) + 127
    byte = np.clip(np.where(amax > 0, byte, 1), 1, 254)
    scaled = (w * np.exp2(127.0 - byte)[:, None, :]).reshape(k, n).astype(np.float32)
    by_word = np.ascontiguousarray(scaled.reshape(k // 512, 128, 4, n).transpose(0, 1, 3, 2))
    if fmt == "e4m3":
        words = by_word.astype(ml_dtypes.float8_e4m3fn).view(np.uint8)
    else:
        c = by_word.astype(ml_dtypes.float4_e2m1fn).view(np.uint8) & 0xF
        words = (c[..., 0::2] | (c[..., 1::2] << 4)).reshape(k // 512, 128, 2 * n)
    return np.ascontiguousarray(words), np.ascontiguousarray(byte.astype(np.uint8).reshape(k // 512, 16, n))


def unpack_weight(words, scales, fmt):
    g, _, n = scales.shape
    words = np.ascontiguousarray(words).reshape(g, 128, n, -1)
    if fmt == "e4m3":
        vals = words.view(ml_dtypes.float8_e4m3fn).astype(np.float64)
    else:
        nib = np.empty((g, 128, n, 4), np.uint8)
        nib[..., 0::2] = words & 0xF
        nib[..., 1::2] = words >> 4
        vals = E2M1[nib]
    vals = vals * np.repeat(np.exp2(scales.astype(np.float64) - 127.0), 8, axis=1)[..., None]
    return vals.transpose(0, 1, 3, 2).reshape(g * 512, n)


def gelu(v):
    return 0.5 * v * (1.0 + np.tanh(np.sqrt(2.0 / np.pi) * (v + 0.044715 * v**3)))


def bf(x):
    return np.asarray(x, np.float32).astype(ml_dtypes.bfloat16)


def planes(Y):
    n, m = Y.shape
    b = f64(bf(Y)).reshape(n // 32, 32, m)
    amax = np.abs(b).max(1)
    byte = np.clip(np.where(amax > 0, np.frexp(amax)[1] - 1 + 127 - 7, 1), 1, 254)
    codes = (b * np.exp2(127.0 - byte)[:, None, :]).reshape(n, m).astype(np.float32).astype(ml_dtypes.float8_e4m3fn).view(np.uint8)
    words = codes.reshape(n // 512, 128, 4, m).transpose(0, 1, 3, 2)
    return np.ascontiguousarray(words), np.ascontiguousarray(byte.astype(np.uint8).reshape(n // 512, 16, m))


K, K2, H, N, T, S = 512, 1024, 1024, 512, 4096, 1024


def setup_inputs():
    n = np.random.standard_normal
    s = mx_kscale(K)[:, None]
    s2 = mx_kscale(K2)[:, None]
    u = mx_kscale(H)[:, None]
    d = {}
    d["tab_words"], d["tab_scales"] = pack_weight(n((K, T)) * s, "e4m3")
    d["offs"] = striped(np.random.permutation(T)[:S])
    d["xs_words"], d["xs_scales"] = pack_weight(n((K2, S)) * s2, "e4m3")
    d["wa"] = (n((K, H)) / K ** 0.5 / s * u.T).astype(np.float32)
    d["wb_words"], d["wb_scales"] = pack_weight(n((K, H)) / K ** 0.5 / s * u.T, "e2m1")
    d["wx"] = (n((K2, H)) / K2 ** 0.5 / s2).astype(np.float32)
    d["span"] = np.random.uniform(1.6, 2.8, H).astype(np.float32)
    d["wo"] = (n((H, N)) / H ** 0.5 / u * np.exp(0.8 * n(N))).astype(np.float32)
    return d


def reference(tab_words, tab_scales, offs, xs_words, xs_scales, wa, wb_words, wb_scales, wx, span, wo):
    v = unpack_weight(tab_words, tab_scales, "e4m3")[:, unstriped(offs)]
    xs = unpack_weight(xs_words, xs_scales, "e4m3")
    wb = unpack_weight(wb_words, wb_scales, "e2m1")
    shape = mxq(f64(wa), 0, "e4m3").T @ v
    motion = wb.T @ v
    hand = mxq(f64(wx), 0, "e4m3").T @ xs
    theta = f64(span)[:, None] * np.tanh(hand)
    h = shape * np.cos(theta) + motion * np.sin(theta)
    y = mxq(f64(wo), 0, "e4m3").T @ mxq(h, 0, "e4m3")
    words, scales = planes(y)
    return y, words, scales

@@ -1,0 +1,368 @@
+import math
+from contextlib import ExitStack
+
+import concourse.mybir as mybir
+
+K, K2, H, N, T, S = 512, 1024, 1024, 512, 4096, 1024
+FLOPS = 2 * S * (2 * K * H + K2 * H + H * N)
+
+F32 = mybir.dt.float32
+BF16 = mybir.dt.bfloat16
+I32 = mybir.dt.int32
+U32 = mybir.dt.uint32
+U16 = mybir.dt.uint16
+U8 = mybir.dt.uint8
+FP8X4 = mybir.dt.float8_e4m3fn_x4
+FP4X4 = mybir.dt.float4_e2m1fn_x4
+ACT = mybir.ActivationFunctionType
+ALU = mybir.AluOpType
+
+P = 128
+PACK = 4
+KP = P * PACK
+HALF = 512
+ABS_ON_VECTOR = ()
+CAST_ON_SCALAR = ("wx00", "wx01", "wa1", "wo0")
+RAW_SLOT = {"wx00": "r0", "wx10": "r1", "wa0": "r2", "wx01": "r0", "wx11": "r2", "wa1": "r0", "wo0": "r2", "wo1": "r0"}
+TANH_SLOT = {2: "r0"}
+Y_CHUNKS = (256, 256)
+
+
+def tile_list_sign_caption_ranker_kernel(
+    tc, tab_words, tab_scales, offs, xs_words, xs_scales, wa, wb_words, wb_scales, wx, span, wo, out_0, out_1, out_2
+):
+    nc = tc.nc
+    with ExitStack() as ctx:
+        keep = ctx.enter_context(tc.tile_pool(name="keep", bufs=1))
+        ring = ctx.enter_context(tc.tile_pool(name="ring", bufs=2))
+        psum = ctx.enter_context(tc.psum_pool(name="psum", bufs=1))
+        reuse = ctx.enter_context(tc.tile_pool(name="reuse", bufs=1))
+
+        offsets = keep.tile([P, S // 16], U16, name="offsets")
+        xs_sc = keep.tile([P, S], U8, name="xs_sc", align_bytes=64)
+        tab_sc = keep.tile([P, T], U8, name="tab_sc", align_bytes=64)
+        wb_sc = keep.tile([P, H], U8, name="wb_sc", align_bytes=64)
+        tab_w = reuse.tile([P, T], I32, name="tab_w", align_bytes=64, offset=4096)
+        wb_w = keep.tile([P, 2 * H], U8, name="wb_w", align_bytes=64)
+        span_t = keep.tile([P, 2, PACK], F32, name="span_t")
+        nspan_t = keep.tile([P, 2, PACK], F32, name="nspan_t")
+        zero_in = keep.tile([P, 1], F32, name="zero_in")
+        zero_b = keep.tile([P, 1], F32, name="zero_b")
+        one = keep.tile([P, 1], F32, name="one")
+        half_pi = keep.tile([P, 1], F32, name="half_pi")
+
+        nc.vector.memset(zero_in[:], 0.0)
+        nc.scalar.activation(zero_b[:], zero_in[:], ACT.Silu)
+        nc.vector.memset(xs_sc[:].bitcast(I32), 0)
+        nc.vector.memset(tab_sc[:].bitcast(I32), 0)
+        nc.vector.memset(wb_sc[:].bitcast(I32), 0)
+        nc.vector.memset(one[:], 1.0)
+        nc.vector.tensor_scalar(half_pi[:], one[:], math.pi / 2, None, ALU.mult)
+
+        def load_weight(w, rows, cols, name):
+            raw = keep.tile([P, PACK, KP], F32, name=name, tag=RAW_SLOT[name])
+            nc.sync.dma_start(raw[:], w[rows : rows + KP, cols : cols + KP].rearrange("(p j) c -> p j c", j=PACK))
+            return raw
+
+        def load_xs(h):
+            xw = keep.tile([P, 2, HALF], I32, name=f"xs_w{h}", align_bytes=64)
+            src = xs_words[:, :, h * HALF : (h + 1) * HALF, :].rearrange("a p c i -> p a (c i)")
+            nc.sync.dma_start(xw[:], src.bitcast(I32))
+            return xw
+
+        sq = nc.sync
+        raws = {}
+        xs_w = {}
+        raws["wx00"] = load_weight(wx, 0, 0, "wx00")
+        for q in range(4):
+            nc.sync.dma_start(xs_sc[32 * q : 32 * q + 8, :].bitcast(I32), xs_scales[:, 4 * q : 4 * q + 4, :].bitcast(I32))
+        raws["wx10"] = load_weight(wx, KP, 0, "wx10")
+        xs_w[0] = load_xs(0)
+        nc.sync.dma_start(span_t[:], span.rearrange("(g p t) -> p g t", g=2, t=PACK))
+        nc.sync.dma_start(wb_w[:].bitcast(I32), wb_words[0].bitcast(I32))
+        nc.sync.dma_start(offsets[:], offs)
+        for q in range(4):
+            sq.dma_start(tab_sc[32 * q : 32 * q + 4, :].bitcast(I32), tab_scales[0, 4 * q : 4 * q + 4, :].bitcast(I32))
+        nc.sync.dma_start(tab_w[:], tab_words[0].rearrange("p n i -> p (n i)").bitcast(I32))
+        for q in range(4):
+            sq.dma_start(wb_sc[32 * q : 32 * q + 4, :].bitcast(I32), wb_scales[0, 4 * q : 4 * q + 4, :].bitcast(I32))
+        raws["wa0"] = load_weight(wa, 0, 0, "wa0")
+        xs_w[1] = load_xs(1)
+
+        nc.vector.tensor_scalar(nspan_t[:], span_t[:], -1.0, None, ALU.mult)
+
+        grouped = {}
+        quant = {}
+
+        def cast(name):
+            if name == "wx10":
+                g = reuse.tile([P, PACK * KP], BF16, name="g_" + name, align_bytes=64, offset=0)
+            elif name == "wa0":
+                g = reuse.tile([P, PACK * KP], BF16, name="g_" + name, align_bytes=64, offset=4096)
+            else:
+                g = ring.tile([P, PACK * KP], BF16, name="g_" + name, tag="grouped", bufs=3, align_bytes=64)
+            dst = g[:].rearrange("p (t m j) -> p m j t", t=PACK, j=PACK)
+            src = raws[name][:].rearrange("p j (m t) -> p m j t", t=PACK)
+            if name in CAST_ON_SCALAR:
+                nc.scalar.copy(dst, src)
+            else:
+                nc.vector.tensor_copy(dst, src)
+            grouped[name] = g
+
+        def quantise(name):
+            codes = keep.tile([P, KP], U32, name="c_" + name, align_bytes=64)
+            scales = keep.tile([P, KP], U8, name="s_" + name, align_bytes=64)
+            nc.vector.quantize_mx(codes[:].bitcast(FP8X4), scales[:], grouped[name][:])
+            quant[name] = (codes, scales)
+
+        wb_wd = reuse.tile([P, 2 * H], U8, name="wb_wd", align_bytes=64, offset=0)
+        wb_sd = reuse.tile([P, H], U8, name="wb_sd", align_bytes=64, offset=3072)
+
+        def deal_wb_words():
+            nc.vector.tensor_copy(
+                wb_wd[:].rearrange("p (g t m b) -> p g m t b", g=2, t=PACK, b=2),
+                wb_w[:].rearrange("p (g m t b) -> p g m t b", g=2, t=PACK, b=2),
+            )
+
+        def deal_wb_scales():
+            nc.vector.tensor_copy(
+                wb_sd[:].rearrange("p (g t m) -> p g m t", g=2, t=PACK),
+                wb_sc[:].rearrange("p (g m t) -> p g m t", g=2, t=PACK),
+            )
+
+        v_w = keep.tile([P, S], U32, name="v_w", align_bytes=64)
+        v_s = reuse.tile([P, S], U8, name="v_s", align_bytes=64, offset=2048)
+
+        def gather_words():
+            nc.vector.tensor_copy(v_w[:], tab_w[:].bitcast(U32).indirect(offsets[:]))
+
+        def gather_scales():
+            nc.vector.tensor_copy(v_s[:], tab_sc[:].indirect(offsets[:]))
+
+        cos_t = {}
+        sin_t = {}
+        tanh_t = {}
+        abs_t = {}
+
+        def open_block(b):
+            cos_t[b] = ring.tile([P, PACK, HALF], F32, name=f"cos{b}", tag="cos", bufs=3)
+            sin_t[b] = ring.tile([P, PACK, HALF], F32, name=f"sin{b}", tag="sin", bufs=3)
+
+        def angle_a(u):
+            b, t = divmod(u, PACK)
+            g, h = divmod(b, 2)
+            cols = slice(t * P, (t + 1) * P)
+            bank = psum.tile([P, HALF], F32, name="hand", tag=f"bank{2 + u if u < 4 else u % 2}")
+            for a in range(2):
+                codes, scales = quant[f"wx{a}{g}"]
+                nc.tensor.matmul_mx(
+                    bank[:],
+                    lhsT=codes[:, cols].bitcast(FP8X4),
+                    lhsT_scale=scales[:, cols],
+                    rhs=xs_w[h][:, a, :].bitcast(FP8X4),
+                    rhs_scale=xs_sc[4 * a : P, h * HALF : (h + 1) * HALF],
+                    start=(a == 0),
+                    stop=(a == 1),
+                )
+            if u in TANH_SLOT:
+                tanh_t[u] = keep.tile([P, HALF], F32, name=f"tanh{u}", tag=TANH_SLOT[u])
+            else:
+                tanh_t[u] = ring.tile([P, HALF], F32, name=f"tanh{u}", tag="tanh", bufs=3)
+            nc.scalar.activation(tanh_t[u][:], bank[:], ACT.Tanh, bias=zero_b[:])
+
+        def angle_b(u):
+            b, t = divmod(u, PACK)
+            g = b // 2
+            abs_t[u] = ring.tile([P, HALF], F32, name=f"abs{u}", tag="abs", bufs=3)
+            if u in ABS_ON_VECTOR:
+                nc.vector.scalar_tensor_tensor(abs_t[u][:], tanh_t[u][:], -1.0, tanh_t[u][:], ALU.mult, ALU.max)
+            else:
+                nc.scalar.activation(abs_t[u][:], tanh_t[u][:], ACT.Abs)
+            nc.scalar.activation(sin_t[b][:, t, :], tanh_t[u][:], ACT.Sin, scale=span_t[:, g, t : t + 1])
+
+        def angle_c(u):
+            b, t = divmod(u, PACK)
+            g = b // 2
+            nc.scalar.activation(
+                cos_t[b][:, t, :], abs_t[u][:], ACT.Sin, scale=nspan_t[:, g, t : t + 1], bias=half_pi[:]
+            )
+
+        def products(u):
+            b, t = divmod(u, PACK)
+            g, h = divmod(b, 2)
+            cols = slice(t * P, (t + 1) * P)
+            motion = psum.tile([P, HALF], F32, name="motion", tag=f"bank{2 + 2 * (u % 2)}")
+            c0 = g * KP + t * P
+            nc.tensor.matmul_mx(
+                motion[:],
+                lhsT=wb_wd[:, 2 * c0 : 2 * (c0 + P)].bitcast(FP4X4),
+                lhsT_scale=wb_sd[:, c0 : c0 + P],
+                rhs=v_w[:, h * HALF : (h + 1) * HALF].bitcast(FP8X4),
+                rhs_scale=v_s[:, h * HALF : (h + 1) * HALF],
+                start=True,
+                stop=True,
+            )
+            shape = psum.tile([P, HALF], F32, name="shape", tag=f"bank{3 + 2 * (u % 2)}")
+            codes, scales = quant[f"wa{g}"]
+            nc.tensor.matmul_mx(
+                shape[:],
+                lhsT=codes[:, cols].bitcast(FP8X4),
+                lhsT_scale=scales[:, cols],
+                rhs=v_w[:, h * HALF : (h + 1) * HALF].bitcast(FP8X4),
+                rhs_scale=v_s[:, h * HALF : (h + 1) * HALF],
+                start=True,
+                stop=True,
+            )
+            nc.vector.tensor_tensor(sin_t[b][:, t, :], motion[:], sin_t[b][:, t, :], ALU.mult)
+            nc.vector.tensor_tensor(cos_t[b][:, t, :], shape[:], cos_t[b][:, t, :], ALU.mult)
+
+        h_bf = {}
+        h_q = {}
+
+        def add_h(b, c0, w):
+            hb = ring.tile([P, PACK * w], BF16, name=f"hb{b}_{c0}", tag="hb", bufs=2, align_bytes=64)
+            nc.vector.tensor_tensor(
+                hb[:].rearrange("p (c i t) -> p c t i", i=4, t=PACK),
+                cos_t[b][:, :, c0 : c0 + w].rearrange("p t (c i) -> p c t i", i=4),
+                sin_t[b][:, :, c0 : c0 + w].rearrange("p t (c i) -> p c t i", i=4),
+                ALU.add,
+            )
+            h_bf[b, c0] = hb
+
+        def quantise_h(b, c0, w):
+            codes = keep.tile([P, w], U32, name=f"hc{b}_{c0}", align_bytes=64)
+            scales = keep.tile([P, w], U8, name=f"hs{b}_{c0}", align_bytes=64)
+            nc.vector.quantize_mx(codes[:].bitcast(FP8X4), scales[:], h_bf[b, c0][:])
+            h_q[b, c0] = (codes, scales)
+
+        y_sc = keep.tile([P, S], U8, name="y_sc", align_bytes=64)
+        y_f = {}
+        y_bf = {}
+        out_rows = out_0.rearrange("(p t) j -> p t j", t=PACK)
+        out_words = out_1[0].rearrange("p m t -> p (m t)").bitcast(I32)
+
+        def y_product(j0, w, banks):
+            h, c0 = divmod(j0, HALF)
+            yt = keep.tile([P, PACK, w], F32, name=f"y{j0}")
+            per_bank = HALF // w
+            for t0 in range(0, PACK, per_bank):
+                bank = psum.tile([P, per_bank, w], F32, name="ybank", tag=f"bank{banks[(t0 // per_bank) % 2]}")
+                for i in range(per_bank):
+                    cols = slice((t0 + i) * P, (t0 + i + 1) * P)
+                    for g in range(2):
+                        codes, scales = quant[f"wo{g}"]
+                        if g == 0:
+                            hc, hs = h_q[h, 0]
+                            rhs, rhs_s = hc[:, c0 : c0 + w], hs[:, c0 : c0 + w]
+                        else:
+                            hc, hs = h_q[2 + h, c0]
+                            rhs, rhs_s = hc[:], hs[:]
+                        nc.tensor.matmul_mx(
+                            bank[:, i, :],
+                            lhsT=codes[:, cols].bitcast(FP8X4),
+                            lhsT_scale=scales[:, cols],
+                            rhs=rhs.bitcast(FP8X4),
+                            rhs_scale=rhs_s,
+                            start=(g == 0),
+                            stop=(g == 1),
+                        )
+                nc.scalar.copy(yt[:, t0 : t0 + per_bank, :], bank[:])
+            nc.sync.dma_start(out_rows[:, :, j0 : j0 + w], yt[:])
+            y_f[j0] = yt
+
+        def y_round(j0, w):
+            yb = ring.tile([P, PACK * w], BF16, name=f"yb{j0}", tag="yb", bufs=2, align_bytes=64)
+            nc.vector.tensor_copy(
+                yb[:].rearrange("p (c i t) -> p c t i", i=4, t=PACK),
+                y_f[j0][:].rearrange("p t (c i) -> p c t i", i=4),
+            )
+            y_bf[j0] = yb
+
+        def y_quantise(j0, w):
+            codes = keep.tile([P, w], I32, name=f"yc{j0}", align_bytes=64)
+            nc.vector.quantize_mx(codes[:].bitcast(FP8X4), y_sc[:, j0 : j0 + w], y_bf[j0][:])
+            nc.sync.dma_start(out_words[:, j0 : j0 + w], codes[:])
+
+        def angles(u):
+            if u % PACK == 0:
+                open_block(u // PACK)
+            angle_a(u)
+            if u >= 1:
+                angle_c(u - 1)
+            angle_b(u)
+
+        cast("wx00")
+        cast("wx10")
+        quantise("wx00")
+        quantise("wx10")
+        deal_wb_words()
+        gather_scales()
+        for u in range(0, 5):
+            angles(u)
+        raws["wx01"] = load_weight(wx, 0, KP, "wx01")
+        gather_words()
+        deal_wb_scales()
+        cast("wa0")
+        raws["wx11"] = load_weight(wx, KP, KP, "wx11")
+        quantise("wa0")
+        cast("wx01")
+        raws["wa1"] = load_weight(wa, 0, KP, "wa1")
+        for u in range(0, 3):
+            products(u)
+            angles(u + 5)
+        products(3)
+        cast("wx11")
+        raws["wo0"] = load_weight(wo, 0, 0, "wo0")
+        quantise("wx01")
+        add_h(0, 0, HALF)
+        quantise("wx11")
+        angles(8)
+        products(4)
+        quantise_h(0, 0, HALF)
+        angles(9)
+        products(5)
+        cast("wa1")
+        raws["wo1"] = load_weight(wo, KP, 0, "wo1")
+        angles(10)
+        products(6)
+        quantise("wa1")
+        cast("wo0")
+        angles(11)
+        products(7)
+        add_h(1, 0, HALF)
+        angles(12)
+        products(8)
+        quantise_h(1, 0, HALF)
+        angles(13)
+        products(9)
+        cast("wo1")
+        quantise("wo0")
+        angles(14)
+        products(10)
+        quantise("wo1")
+        angles(15)
+        products(11)
+        angle_c(15)
+        add_h(2, 0, HALF)
+        products(12)
+        quantise_h(2, 0, HALF)
+        y_product(0, HALF, (6, 7))
+        products(13)
+        products(14)
+        y_round(0, HALF)
+        products(15)
+        y_quantise(0, HALF)
+        c0 = 0
+        for i, w in enumerate(Y_CHUNKS):
+            add_h(3, c0, w)
+            quantise_h(3, c0, w)
+            y_product(HALF + c0, w, ((0, 1), (6, 7))[i % 2])
+            c0 = c0 + w
+        c0 = 0
+        for w in Y_CHUNKS:
+            y_round(HALF + c0, w)
+            y_quantise(HALF + c0, w)
+            c0 = c0 + w
+
+        for q in range(4):
+            nc.sync.dma_start(out_2[0, 4 * q : 4 * q + 4, :].bitcast(I32), y_sc[32 * q : 32 * q + 4, :].bitcast(I32))

@@ -19,13 +19,65 @@ ALU = mybir.AluOpType
 
 P = 128
 PACK = 4
-KP = P * PACK
-HALF = 512
-ABS_ON_VECTOR = ()
-CAST_ON_SCALAR = ("wx00", "wx01", "wa1", "wo0")
-RAW_SLOT = {"wx00": "r0", "wx10": "r1", "wa0": "r2", "wx01": "r0", "wx11": "r2", "wa1": "r0", "wo0": "r2", "wo1": "r0"}
-TANH_SLOT = {2: "r0"}
-Y_CHUNKS = (256, 256)
+PASS = P * PACK
+BANK = 512
+HALF = S // 2
+QUARTER = S // 4
+LAST = S // 8
+RUN = 4
+
+BLOCKS = ((0, 0, HALF), (0, HALF, HALF), (1, 0, HALF), (1, HALF, QUARTER), (1, HALF + QUARTER, QUARTER))
+UNITS = [(b, t) for b, (g, j0, w) in enumerate(BLOCKS) for t in range(0, PACK, BANK // w)]
+
+ROUNDED_ON_SCALAR = ("wx11", "wo0")
+WX10_VECTOR_SHARE = 88
+PAIRS = {"wx01": ("wx_g1", 0), "wx11": ("wx_g1", 1), "wo0": ("wo", 0), "wo1": ("wo", 1)}
+
+PIECE_BF16 = PASS * PACK * 2
+PIECE_F32 = PASS * PACK * 4
+TABLE_AT = PIECE_BF16
+RAW_AT = [TABLE_AT + 4 * T + i * PIECE_F32 for i in range(4)]
+SHARED = {
+    "round_wx00": 0,
+    "round_wx10": 0,
+    "v_scales0": 0,
+    "v_scales1": HALF,
+    "wb_dealt": S,
+    "wb_scales_dealt": S + 2 * H,
+    "tab_w": TABLE_AT,
+    "round_wa0": TABLE_AT,
+    "round_wx_g1": TABLE_AT + PIECE_BF16,
+    "round_wo": TABLE_AT,
+    "wx00": RAW_AT[0],
+    "tanh2": RAW_AT[0],
+    "wx01": RAW_AT[0],
+    "wx10": RAW_AT[1],
+    "tanh1": RAW_AT[1],
+    "wa0": RAW_AT[1],
+    "wo0": RAW_AT[1],
+    "tanh3": RAW_AT[2],
+    "wx11": RAW_AT[2],
+    "wo1": RAW_AT[2],
+    "tanh4": RAW_AT[3],
+    "wa1": RAW_AT[3],
+}
+
+OUT_BANKS = (6, 7)
+LAST_BANKS = (4, 5)
+
+
+def hand_bank(u):
+    return u % 4 if u < 6 else 4 + u % 2
+
+
+def motion_bank(u):
+    if u < 4:
+        return 4 + u
+    return (0, 2, 6)[(u - 4) % 3] if u < 10 else 2 * (u % 2)
+
+
+def shape_bank(u):
+    return (2, 3, 6, 7)[u] if u < 4 else motion_bank(u) + 1
 
 
 def tile_list_sign_caption_ranker_kernel(
@@ -34,335 +86,401 @@ def tile_list_sign_caption_ranker_kernel(
     nc = tc.nc
     with ExitStack() as ctx:
         keep = ctx.enter_context(tc.tile_pool(name="keep", bufs=1))
-        ring = ctx.enter_context(tc.tile_pool(name="ring", bufs=2))
-        psum = ctx.enter_context(tc.psum_pool(name="psum", bufs=1))
+        ring = ctx.enter_context(tc.tile_pool(name="ring", bufs=3))
         reuse = ctx.enter_context(tc.tile_pool(name="reuse", bufs=1))
+        psum = ctx.enter_context(tc.psum_pool(name="psum", bufs=1))
+
+        def place(shape, dtype, name):
+            if name in SHARED:
+                return reuse.tile(shape, dtype, name=name, align_bytes=64, offset=SHARED[name])
+            return keep.tile(shape, dtype, name=name, align_bytes=64)
+
+        def bank_tile(number, slices, width):
+            return psum.tile([P, slices, width], F32, name="bank", tag=f"bank{number}")
+
+        def mx(out, lhs, lhs_scale, rhs, rhs_scale, start, stop, lhs_dtype=FP8X4):
+            nc.tensor.matmul_mx(
+                out,
+                lhsT=lhs.bitcast(lhs_dtype),
+                lhsT_scale=lhs_scale,
+                rhs=rhs.bitcast(FP8X4),
+                rhs_scale=rhs_scale,
+                start=start,
+                stop=stop,
+            )
+
+        def interleaved(tile):
+            return tile.rearrange("p (c i t) -> p c t i", i=RUN, t=PACK)
+
+        def by_slices(view):
+            return view.rearrange("p t (c i) -> p c t i", i=RUN)
 
         offsets = keep.tile([P, S // 16], U16, name="offsets")
-        xs_sc = keep.tile([P, S], U8, name="xs_sc", align_bytes=64)
-        tab_sc = keep.tile([P, T], U8, name="tab_sc", align_bytes=64)
-        wb_sc = keep.tile([P, H], U8, name="wb_sc", align_bytes=64)
-        tab_w = reuse.tile([P, T], I32, name="tab_w", align_bytes=64, offset=4096)
-        wb_w = keep.tile([P, 2 * H], U8, name="wb_w", align_bytes=64)
+        xs_sc = place([P, S], U8, "xs_sc")
+        tab_sc = place([P, T], U8, "tab_sc")
+        wb_sc = place([P, H], U8, "wb_sc")
+        tab_w = place([P, T], I32, "tab_w")
+        wb_w = place([P, 2 * H], U8, "wb_w")
         span_t = keep.tile([P, 2, PACK], F32, name="span_t")
-        nspan_t = keep.tile([P, 2, PACK], F32, name="nspan_t")
-        zero_in = keep.tile([P, 1], F32, name="zero_in")
-        zero_b = keep.tile([P, 1], F32, name="zero_b")
+        minus_span = keep.tile([P, 2, PACK], F32, name="minus_span")
+        zero = keep.tile([P, 1], F32, name="zero")
+        tanh_bias = keep.tile([P, 1], F32, name="tanh_bias")
         one = keep.tile([P, 1], F32, name="one")
         half_pi = keep.tile([P, 1], F32, name="half_pi")
 
-        nc.vector.memset(zero_in[:], 0.0)
-        nc.scalar.activation(zero_b[:], zero_in[:], ACT.Silu)
+        nc.vector.memset(zero[:], 0.0)
+        nc.scalar.activation(tanh_bias[:], zero[:], ACT.Silu)
         nc.vector.memset(xs_sc[:].bitcast(I32), 0)
         nc.vector.memset(tab_sc[:].bitcast(I32), 0)
         nc.vector.memset(wb_sc[:].bitcast(I32), 0)
         nc.vector.memset(one[:], 1.0)
         nc.vector.tensor_scalar(half_pi[:], one[:], math.pi / 2, None, ALU.mult)
 
-        def load_weight(w, rows, cols, name):
-            raw = keep.tile([P, PACK, KP], F32, name=name, tag=RAW_SLOT[name])
-            nc.sync.dma_start(raw[:], w[rows : rows + KP, cols : cols + KP].rearrange("(p j) c -> p j c", j=PACK))
-            return raw
-
-        def load_xs(h):
-            xw = keep.tile([P, 2, HALF], I32, name=f"xs_w{h}", align_bytes=64)
-            src = xs_words[:, :, h * HALF : (h + 1) * HALF, :].rearrange("a p c i -> p a (c i)")
-            nc.sync.dma_start(xw[:], src.bitcast(I32))
-            return xw
-
-        sq = nc.sync
-        raws = {}
+        loaded = {}
         xs_w = {}
-        raws["wx00"] = load_weight(wx, 0, 0, "wx00")
-        for q in range(4):
-            nc.sync.dma_start(xs_sc[32 * q : 32 * q + 8, :].bitcast(I32), xs_scales[:, 4 * q : 4 * q + 4, :].bitcast(I32))
-        raws["wx10"] = load_weight(wx, KP, 0, "wx10")
-        xs_w[0] = load_xs(0)
+
+        def load_piece(name, weight, row0, col0):
+            loaded[name] = place([P, PACK, PASS], F32, name)
+            rows = weight[row0 : row0 + PASS, col0 : col0 + PASS]
+            nc.sync.dma_start(loaded[name][:], rows.rearrange("(p j) c -> p j c", j=PACK))
+
+        def load_xs(half):
+            xs_w[half] = place([P, 2, HALF], I32, f"xs_w{half}")
+            words = xs_words[:, :, half * HALF : (half + 1) * HALF, :].rearrange("a p c i -> p a (c i)")
+            nc.sync.dma_start(xs_w[half][:], words.bitcast(I32))
+
+        def load_scale_rows(tile, scales):
+            for q in range(4):
+                nc.sync.dma_start(tile[q:P:32, :].bitcast(I32), scales[0, q:16:4, :].bitcast(I32))
+
+        load_piece("wx00", wx, 0, 0)
+        load_piece("wx10", wx, PASS, 0)
+        for quad in range(4):
+            nc.sync.dma_start(
+                xs_sc[32 * quad : 32 * quad + 8, :].bitcast(I32), xs_scales[:, 4 * quad : 4 * quad + 4, :].bitcast(I32)
+            )
+        load_xs(0)
         nc.sync.dma_start(span_t[:], span.rearrange("(g p t) -> p g t", g=2, t=PACK))
-        nc.sync.dma_start(wb_w[:].bitcast(I32), wb_words[0].bitcast(I32))
         nc.sync.dma_start(offsets[:], offs)
-        for q in range(4):
-            sq.dma_start(tab_sc[32 * q : 32 * q + 4, :].bitcast(I32), tab_scales[0, 4 * q : 4 * q + 4, :].bitcast(I32))
+        load_scale_rows(tab_sc, tab_scales)
+        nc.sync.dma_start(wb_w[:].bitcast(I32), wb_words[0].bitcast(I32))
+        load_scale_rows(wb_sc, wb_scales)
         nc.sync.dma_start(tab_w[:], tab_words[0].rearrange("p n i -> p (n i)").bitcast(I32))
-        for q in range(4):
-            sq.dma_start(wb_sc[32 * q : 32 * q + 4, :].bitcast(I32), wb_scales[0, 4 * q : 4 * q + 4, :].bitcast(I32))
-        raws["wa0"] = load_weight(wa, 0, 0, "wa0")
-        xs_w[1] = load_xs(1)
+        load_xs(1)
 
-        nc.vector.tensor_scalar(nspan_t[:], span_t[:], -1.0, None, ALU.mult)
+        nc.gpsimd.tensor_scalar(minus_span[:], span_t[:], -1.0, 0.0, ALU.mult, ALU.add)
 
-        grouped = {}
-        quant = {}
+        rounded = {}
+        weight_q = {}
 
-        def cast(name):
-            if name == "wx10":
-                g = reuse.tile([P, PACK * KP], BF16, name="g_" + name, align_bytes=64, offset=0)
-            elif name == "wa0":
-                g = reuse.tile([P, PACK * KP], BF16, name="g_" + name, align_bytes=64, offset=4096)
+        def round_piece(name):
+            if name in PAIRS:
+                pair, i = PAIRS[name]
+                if i == 0:
+                    rounded[pair] = place([P, 2 * PACK * PASS], BF16, "round_" + pair)
+                target = rounded[pair][:, i * PACK * PASS : (i + 1) * PACK * PASS]
             else:
-                g = ring.tile([P, PACK * KP], BF16, name="g_" + name, tag="grouped", bufs=3, align_bytes=64)
-            dst = g[:].rearrange("p (t m j) -> p m j t", t=PACK, j=PACK)
-            src = raws[name][:].rearrange("p j (m t) -> p m j t", t=PACK)
-            if name in CAST_ON_SCALAR:
+                rounded[name] = place([P, PACK * PASS], BF16, "round_" + name)
+                target = rounded[name][:]
+            dst = target.rearrange("p (t m j) -> p m j t", t=PACK, j=PACK)
+            src = loaded[name][:].rearrange("p j (m t) -> p m j t", t=PACK)
+            if name == "wx10":
+                nc.vector.tensor_copy(dst[:, :WX10_VECTOR_SHARE], src[:, :WX10_VECTOR_SHARE])
+                nc.scalar.copy(dst[:, WX10_VECTOR_SHARE:], src[:, WX10_VECTOR_SHARE:])
+            elif name in ROUNDED_ON_SCALAR:
                 nc.scalar.copy(dst, src)
             else:
                 nc.vector.tensor_copy(dst, src)
-            grouped[name] = g
 
-        def quantise(name):
-            codes = keep.tile([P, KP], U32, name="c_" + name, align_bytes=64)
-            scales = keep.tile([P, KP], U8, name="s_" + name, align_bytes=64)
-            nc.vector.quantize_mx(codes[:].bitcast(FP8X4), scales[:], grouped[name][:])
-            quant[name] = (codes, scales)
+        def quantise_weight(name, pieces):
+            codes = place([P, len(pieces) * PASS], U32, "codes_" + name)
+            scales = place([P, len(pieces) * PASS], U8, "scales_" + name)
+            nc.vector.quantize_mx(codes[:].bitcast(FP8X4), scales[:], rounded[name][:])
+            for i, piece in enumerate(pieces):
+                weight_q[piece] = (codes[:, i * PASS : (i + 1) * PASS], scales[:, i * PASS : (i + 1) * PASS])
 
-        wb_wd = reuse.tile([P, 2 * H], U8, name="wb_wd", align_bytes=64, offset=0)
-        wb_sd = reuse.tile([P, H], U8, name="wb_sd", align_bytes=64, offset=3072)
+        wb_dealt = place([P, 2 * H], U8, "wb_dealt")
+        wb_scales_dealt = place([P, H], U8, "wb_scales_dealt")
 
-        def deal_wb_words():
+        def deal_wb():
             nc.vector.tensor_copy(
-                wb_wd[:].rearrange("p (g t m b) -> p g m t b", g=2, t=PACK, b=2),
+                wb_dealt[:].rearrange("p (g t m b) -> p g m t b", g=2, t=PACK, b=2),
                 wb_w[:].rearrange("p (g m t b) -> p g m t b", g=2, t=PACK, b=2),
             )
-
-        def deal_wb_scales():
             nc.vector.tensor_copy(
-                wb_sd[:].rearrange("p (g t m) -> p g m t", g=2, t=PACK),
+                wb_scales_dealt[:].rearrange("p (g t m) -> p g m t", g=2, t=PACK),
                 wb_sc[:].rearrange("p (g m t) -> p g m t", g=2, t=PACK),
             )
 
-        v_w = keep.tile([P, S], U32, name="v_w", align_bytes=64)
-        v_s = reuse.tile([P, S], U8, name="v_s", align_bytes=64, offset=2048)
+        v_words = [place([P, HALF], U32, f"v_words{half}") for half in range(2)]
+        v_scales = [place([P, HALF], U8, f"v_scales{half}") for half in range(2)]
 
-        def gather_words():
-            nc.vector.tensor_copy(v_w[:], tab_w[:].bitcast(U32).indirect(offsets[:]))
-
-        def gather_scales():
-            nc.vector.tensor_copy(v_s[:], tab_sc[:].indirect(offsets[:]))
+        def gather(targets, window):
+            for half in range(2):
+                entries = offsets[:, half * HALF // 16 : (half + 1) * HALF // 16]
+                nc.vector.tensor_copy(targets[half][:], window.indirect(entries))
 
         cos_t = {}
         sin_t = {}
         tanh_t = {}
         abs_t = {}
 
-        def open_block(b):
-            cos_t[b] = ring.tile([P, PACK, HALF], F32, name=f"cos{b}", tag="cos", bufs=3)
-            sin_t[b] = ring.tile([P, PACK, HALF], F32, name=f"sin{b}", tag="sin", bufs=3)
+        def unit(u):
+            b, t0 = UNITS[u]
+            g, j0, w = BLOCKS[b]
+            return b, g, j0, w, range(t0, t0 + BANK // w)
 
-        def angle_a(u):
-            b, t = divmod(u, PACK)
-            g, h = divmod(b, 2)
-            cols = slice(t * P, (t + 1) * P)
-            bank = psum.tile([P, HALF], F32, name="hand", tag=f"bank{2 + u if u < 4 else u % 2}")
-            for a in range(2):
-                codes, scales = quant[f"wx{a}{g}"]
-                nc.tensor.matmul_mx(
-                    bank[:],
-                    lhsT=codes[:, cols].bitcast(FP8X4),
-                    lhsT_scale=scales[:, cols],
-                    rhs=xs_w[h][:, a, :].bitcast(FP8X4),
-                    rhs_scale=xs_sc[4 * a : P, h * HALF : (h + 1) * HALF],
-                    start=(a == 0),
-                    stop=(a == 1),
+        def cosine(u):
+            b, g, j0, w, slices = unit(u)
+            for i, t in enumerate(slices):
+                nc.scalar.activation(
+                    cos_t[b][:, t, :], abs_t[u][:, i, :], ACT.Sin, scale=minus_span[:, g, t : t + 1], bias=half_pi[:]
                 )
-            if u in TANH_SLOT:
-                tanh_t[u] = keep.tile([P, HALF], F32, name=f"tanh{u}", tag=TANH_SLOT[u])
-            else:
-                tanh_t[u] = ring.tile([P, HALF], F32, name=f"tanh{u}", tag="tanh", bufs=3)
-            nc.scalar.activation(tanh_t[u][:], bank[:], ACT.Tanh, bias=zero_b[:])
 
-        def angle_b(u):
-            b, t = divmod(u, PACK)
-            g = b // 2
-            abs_t[u] = ring.tile([P, HALF], F32, name=f"abs{u}", tag="abs", bufs=3)
-            if u in ABS_ON_VECTOR:
-                nc.vector.scalar_tensor_tensor(abs_t[u][:], tanh_t[u][:], -1.0, tanh_t[u][:], ALU.mult, ALU.max)
+        def angles(u):
+            b, g, j0, w, slices = unit(u)
+            if slices[0] == 0:
+                cos_t[b] = ring.tile([P, PACK, w], F32, name=f"cos{b}", tag="cos", bufs=4)
+                sin_t[b] = ring.tile([P, PACK, w], F32, name=f"sin{b}", tag="sin", bufs=4)
+            hand = bank_tile(hand_bank(u), len(slices), w)
+            half, c0 = divmod(j0, HALF)
+            for i, t in enumerate(slices):
+                for a in (1, 0):
+                    codes, scales = weight_q[f"wx{a}{g}"]
+                    mx(
+                        hand[:, i, :],
+                        codes[:, t * P : (t + 1) * P],
+                        scales[:, t * P : (t + 1) * P],
+                        xs_w[half][:, a, c0 : c0 + w],
+                        xs_sc[4 * a : P, j0 : j0 + w],
+                        start=(a == 1),
+                        stop=(a == 0),
+                    )
+            if f"tanh{u}" in SHARED:
+                tanh_t[u] = place([P, len(slices), w], F32, f"tanh{u}")
             else:
-                nc.scalar.activation(abs_t[u][:], tanh_t[u][:], ACT.Abs)
-            nc.scalar.activation(sin_t[b][:, t, :], tanh_t[u][:], ACT.Sin, scale=span_t[:, g, t : t + 1])
+                tanh_t[u] = ring.tile([P, len(slices), w], F32, name=f"tanh{u}", tag="tanh")
+            nc.scalar.activation(tanh_t[u][:], hand[:], ACT.Tanh, bias=tanh_bias[:])
+            if u >= 1:
+                cosine(u - 1)
+            abs_t[u] = ring.tile([P, len(slices), w], F32, name=f"abs{u}", tag="abs")
+            nc.scalar.activation(abs_t[u][:], tanh_t[u][:], ACT.Abs)
+            for i, t in enumerate(slices):
+                nc.scalar.activation(sin_t[b][:, t, :], tanh_t[u][:, i, :], ACT.Sin, scale=span_t[:, g, t : t + 1])
 
-        def angle_c(u):
-            b, t = divmod(u, PACK)
-            g = b // 2
-            nc.scalar.activation(
-                cos_t[b][:, t, :], abs_t[u][:], ACT.Sin, scale=nspan_t[:, g, t : t + 1], bias=half_pi[:]
-            )
+        def motion_times_sine(u):
+            b, g, j0, w, slices = unit(u)
+            half, c0 = divmod(j0, HALF)
+            motion = bank_tile(motion_bank(u), len(slices), w)
+            for i, t in enumerate(slices):
+                col = g * PASS + t * P
+                mx(
+                    motion[:, i, :],
+                    wb_dealt[:, 2 * col : 2 * (col + P)],
+                    wb_scales_dealt[:, col : col + P],
+                    v_words[half][:, c0 : c0 + w],
+                    v_scales[half][:, c0 : c0 + w],
+                    start=True,
+                    stop=True,
+                    lhs_dtype=FP4X4,
+                )
+            rows = sin_t[b][:, slices[0] : slices[-1] + 1, :]
+            nc.vector.tensor_tensor(rows, motion[:], rows, ALU.mult)
+
+        def shape_times_cosine(u):
+            b, g, j0, w, slices = unit(u)
+            half, c0 = divmod(j0, HALF)
+            shape = bank_tile(shape_bank(u), len(slices), w)
+            codes, scales = weight_q[f"wa{g}"]
+            for i, t in enumerate(slices):
+                mx(
+                    shape[:, i, :],
+                    codes[:, t * P : (t + 1) * P],
+                    scales[:, t * P : (t + 1) * P],
+                    v_words[half][:, c0 : c0 + w],
+                    v_scales[half][:, c0 : c0 + w],
+                    start=True,
+                    stop=True,
+                )
+            rows = cos_t[b][:, slices[0] : slices[-1] + 1, :]
+            nc.vector.tensor_tensor(rows, shape[:], rows, ALU.mult)
 
         def products(u):
-            b, t = divmod(u, PACK)
-            g, h = divmod(b, 2)
-            cols = slice(t * P, (t + 1) * P)
-            motion = psum.tile([P, HALF], F32, name="motion", tag=f"bank{2 + 2 * (u % 2)}")
-            c0 = g * KP + t * P
-            nc.tensor.matmul_mx(
-                motion[:],
-                lhsT=wb_wd[:, 2 * c0 : 2 * (c0 + P)].bitcast(FP4X4),
-                lhsT_scale=wb_sd[:, c0 : c0 + P],
-                rhs=v_w[:, h * HALF : (h + 1) * HALF].bitcast(FP8X4),
-                rhs_scale=v_s[:, h * HALF : (h + 1) * HALF],
-                start=True,
-                stop=True,
-            )
-            shape = psum.tile([P, HALF], F32, name="shape", tag=f"bank{3 + 2 * (u % 2)}")
-            codes, scales = quant[f"wa{g}"]
-            nc.tensor.matmul_mx(
-                shape[:],
-                lhsT=codes[:, cols].bitcast(FP8X4),
-                lhsT_scale=scales[:, cols],
-                rhs=v_w[:, h * HALF : (h + 1) * HALF].bitcast(FP8X4),
-                rhs_scale=v_s[:, h * HALF : (h + 1) * HALF],
-                start=True,
-                stop=True,
-            )
-            nc.vector.tensor_tensor(sin_t[b][:, t, :], motion[:], sin_t[b][:, t, :], ALU.mult)
-            nc.vector.tensor_tensor(cos_t[b][:, t, :], shape[:], cos_t[b][:, t, :], ALU.mult)
+            motion_times_sine(u)
+            shape_times_cosine(u)
 
-        h_bf = {}
+        h_rounded = {}
         h_q = {}
 
         def add_h(b, c0, w):
-            hb = ring.tile([P, PACK * w], BF16, name=f"hb{b}_{c0}", tag="hb", bufs=2, align_bytes=64)
+            tag, bufs = ("h_wide", 1) if w == HALF else ("h_narrow", 3)
+            h_rounded[b, c0] = ring.tile([P, PACK * w], BF16, name=f"hb{b}_{c0}", tag=tag, bufs=bufs, align_bytes=64)
             nc.vector.tensor_tensor(
-                hb[:].rearrange("p (c i t) -> p c t i", i=4, t=PACK),
-                cos_t[b][:, :, c0 : c0 + w].rearrange("p t (c i) -> p c t i", i=4),
-                sin_t[b][:, :, c0 : c0 + w].rearrange("p t (c i) -> p c t i", i=4),
+                interleaved(h_rounded[b, c0][:]),
+                by_slices(cos_t[b][:, :, c0 : c0 + w]),
+                by_slices(sin_t[b][:, :, c0 : c0 + w]),
                 ALU.add,
             )
-            h_bf[b, c0] = hb
 
         def quantise_h(b, c0, w):
-            codes = keep.tile([P, w], U32, name=f"hc{b}_{c0}", align_bytes=64)
-            scales = keep.tile([P, w], U8, name=f"hs{b}_{c0}", align_bytes=64)
-            nc.vector.quantize_mx(codes[:].bitcast(FP8X4), scales[:], h_bf[b, c0][:])
+            codes = place([P, w], U32, f"h_codes{b}_{c0}")
+            scales = place([P, w], U8, f"h_scales{b}_{c0}")
+            nc.vector.quantize_mx(codes[:].bitcast(FP8X4), scales[:], h_rounded[b, c0][:])
             h_q[b, c0] = (codes, scales)
 
-        y_sc = keep.tile([P, S], U8, name="y_sc", align_bytes=64)
-        y_f = {}
-        y_bf = {}
         out_rows = out_0.rearrange("(p t) j -> p t j", t=PACK)
         out_words = out_1[0].rearrange("p m t -> p (m t)").bitcast(I32)
+        y_words = place([P, S], I32, "y_words")
+        y_sc = place([P, S], U8, "y_sc")
+        y_f32 = {}
+        y_rounded = {}
+        last_sums = {}
 
-        def y_product(j0, w, banks):
-            h, c0 = divmod(j0, HALF)
-            yt = keep.tile([P, PACK, w], F32, name=f"y{j0}")
-            per_bank = HALF // w
+        def out_pass(out, t, g, j0, w, b1, start, stop):
+            if g == 0:
+                half, c0 = divmod(j0, HALF)
+                codes, scales = h_q[half, 0]
+                codes, scales = codes[:, c0 : c0 + w], scales[:, c0 : c0 + w]
+            else:
+                codes, scales = h_q[b1, j0 - BLOCKS[b1][1]]
+                codes, scales = codes[:], scales[:]
+            wo_codes, wo_scales = weight_q[f"wo{g}"]
+            mx(out, wo_codes[:, t * P : (t + 1) * P], wo_scales[:, t * P : (t + 1) * P], codes, scales, start, stop)
+
+        def out_block(b1):
+            j0, w = BLOCKS[b1][1:]
+            y_f32[j0] = place([P, PACK, w], F32, f"y{j0}")
+            per_bank = BANK // w
             for t0 in range(0, PACK, per_bank):
-                bank = psum.tile([P, per_bank, w], F32, name="ybank", tag=f"bank{banks[(t0 // per_bank) % 2]}")
+                sums = bank_tile(OUT_BANKS[(t0 // per_bank) % 2], per_bank, w)
                 for i in range(per_bank):
-                    cols = slice((t0 + i) * P, (t0 + i + 1) * P)
                     for g in range(2):
-                        codes, scales = quant[f"wo{g}"]
-                        if g == 0:
-                            hc, hs = h_q[h, 0]
-                            rhs, rhs_s = hc[:, c0 : c0 + w], hs[:, c0 : c0 + w]
-                        else:
-                            hc, hs = h_q[2 + h, c0]
-                            rhs, rhs_s = hc[:], hs[:]
-                        nc.tensor.matmul_mx(
-                            bank[:, i, :],
-                            lhsT=codes[:, cols].bitcast(FP8X4),
-                            lhsT_scale=scales[:, cols],
-                            rhs=rhs.bitcast(FP8X4),
-                            rhs_scale=rhs_s,
-                            start=(g == 0),
-                            stop=(g == 1),
-                        )
-                nc.scalar.copy(yt[:, t0 : t0 + per_bank, :], bank[:])
-            nc.sync.dma_start(out_rows[:, :, j0 : j0 + w], yt[:])
-            y_f[j0] = yt
+                        out_pass(sums[:, i, :], t0 + i, g, j0, w, b1, start=(g == 0), stop=(g == 1))
+                nc.scalar.copy(y_f32[j0][:, t0 : t0 + per_bank, :], sums[:])
+                done = t0 + per_bank
+                if done % 2 == 0:
+                    nc.sync.dma_start(out_rows[:, done - 2 : done, j0 : j0 + w], y_f32[j0][:, done - 2 : done, :])
 
-        def y_round(j0, w):
-            yb = ring.tile([P, PACK * w], BF16, name=f"yb{j0}", tag="yb", bufs=2, align_bytes=64)
-            nc.vector.tensor_copy(
-                yb[:].rearrange("p (c i t) -> p c t i", i=4, t=PACK),
-                y_f[j0][:].rearrange("p t (c i) -> p c t i", i=4),
-            )
-            y_bf[j0] = yb
+        def last_piece_group0(i):
+            j0 = S - QUARTER + i * LAST
+            last_sums[i] = bank_tile(LAST_BANKS[i], PACK, LAST)
+            for t in range(PACK):
+                out_pass(last_sums[i][:, t, :], t, 0, j0, LAST, 4, start=(t == 0), stop=False)
 
-        def y_quantise(j0, w):
-            codes = keep.tile([P, w], I32, name=f"yc{j0}", align_bytes=64)
-            nc.vector.quantize_mx(codes[:].bitcast(FP8X4), y_sc[:, j0 : j0 + w], y_bf[j0][:])
-            nc.sync.dma_start(out_words[:, j0 : j0 + w], codes[:])
+        def last_piece_group1(i):
+            j0 = S - QUARTER + i * LAST
+            for t in range(PACK):
+                out_pass(last_sums[i][:, t, :], t, 1, j0, LAST, 4, start=False, stop=(t == PACK - 1))
+            y_f32[j0] = place([P, PACK, LAST], F32, f"y{j0}")
+            nc.scalar.copy(y_f32[j0][:], last_sums[i][:])
+            nc.sync.dma_start(out_rows[:, :, j0 : j0 + LAST], y_f32[j0][:])
 
-        def angles(u):
-            if u % PACK == 0:
-                open_block(u // PACK)
-            angle_a(u)
-            if u >= 1:
-                angle_c(u - 1)
-            angle_b(u)
+        def round_y(j0, w, copy):
+            source = y_f32[0][:, :, j0 : j0 + w] if j0 < HALF else y_f32[j0][:]
+            y_rounded[j0] = ring.tile([P, PACK * w], BF16, name=f"yb{j0}", tag="y_rounded", bufs=5, align_bytes=64)
+            copy(interleaved(y_rounded[j0][:]), by_slices(source))
 
-        cast("wx00")
-        cast("wx10")
-        quantise("wx00")
-        quantise("wx10")
-        deal_wb_words()
-        gather_scales()
-        for u in range(0, 5):
-            angles(u)
-        raws["wx01"] = load_weight(wx, 0, KP, "wx01")
-        gather_words()
-        deal_wb_scales()
-        cast("wa0")
-        raws["wx11"] = load_weight(wx, KP, KP, "wx11")
-        quantise("wa0")
-        cast("wx01")
-        raws["wa1"] = load_weight(wa, 0, KP, "wa1")
-        for u in range(0, 3):
-            products(u)
-            angles(u + 5)
-        products(3)
-        cast("wx11")
-        raws["wo0"] = load_weight(wo, 0, 0, "wo0")
-        quantise("wx01")
+        def quantise_y(j0, w):
+            nc.vector.quantize_mx(y_words[:, j0 : j0 + w].bitcast(FP8X4), y_sc[:, j0 : j0 + w], y_rounded[j0][:])
+
+        def store_words(j0, w):
+            nc.sync.dma_start(out_words[:, j0 : j0 + w], y_words[:, j0 : j0 + w])
+
+        round_piece("wx00")
+        quantise_weight("wx00", ["wx00"])
+        round_piece("wx10")
+        quantise_weight("wx10", ["wx10"])
+        gather(v_scales, tab_sc[:])
+        angles(0)
+        angles(1)
+        load_piece("wa0", wa, 0, 0)
+        deal_wb()
+        angles(2)
+        load_piece("wx01", wx, 0, PASS)
+        angles(3)
+        load_piece("wx11", wx, PASS, PASS)
+        gather(v_words, tab_w[:].bitcast(U32))
+        angles(4)
+        load_piece("wa1", wa, 0, PASS)
+
+        for u in range(4):
+            motion_times_sine(u)
+        round_piece("wa0")
+        load_piece("wo0", wo, 0, 0)
+        motion_times_sine(4)
+        quantise_weight("wa0", ["wa0"])
+        angles(5)
+        round_piece("wx01")
+        shape_times_cosine(0)
+        shape_times_cosine(1)
+        angles(6)
+        shape_times_cosine(2)
+        shape_times_cosine(3)
+        round_piece("wx11")
+        load_piece("wo1", wo, PASS, 0)
+        angles(7)
+        shape_times_cosine(4)
+        quantise_weight("wx_g1", ["wx01", "wx11"])
         add_h(0, 0, HALF)
-        quantise("wx11")
+
         angles(8)
-        products(4)
+        motion_times_sine(5)
         quantise_h(0, 0, HALF)
+        round_piece("wa1")
+        shape_times_cosine(5)
+        quantise_weight("wa1", ["wa1"])
         angles(9)
-        products(5)
-        cast("wa1")
-        raws["wo1"] = load_weight(wo, KP, 0, "wo1")
-        angles(10)
         products(6)
-        quantise("wa1")
-        cast("wo0")
-        angles(11)
+        round_piece("wo0")
         products(7)
-        add_h(1, 0, HALF)
-        angles(12)
+        angles(10)
         products(8)
-        quantise_h(1, 0, HALF)
-        angles(13)
+        round_piece("wo1")
+        angles(11)
         products(9)
-        cast("wo1")
-        quantise("wo0")
-        angles(14)
+        quantise_weight("wo", ["wo0", "wo1"])
+        angles(12)
         products(10)
-        quantise("wo1")
-        angles(15)
         products(11)
-        angle_c(15)
+
         add_h(2, 0, HALF)
-        products(12)
+        angles(13)
+        motion_times_sine(12)
         quantise_h(2, 0, HALF)
-        y_product(0, HALF, (6, 7))
-        products(13)
-        products(14)
-        y_round(0, HALF)
+        out_block(2)
+        shape_times_cosine(12)
+        add_h(1, 0, HALF)
+        angles(14)
+        motion_times_sine(13)
+        quantise_h(1, 0, HALF)
+        angles(15)
+        cosine(15)
+        shape_times_cosine(13)
+        add_h(3, 0, QUARTER)
+        motion_times_sine(14)
+        quantise_h(3, 0, QUARTER)
+        out_block(3)
+        round_y(0, QUARTER, nc.scalar.copy)
+        round_y(QUARTER, QUARTER, nc.scalar.copy)
+        shape_times_cosine(14)
         products(15)
-        y_quantise(0, HALF)
-        c0 = 0
-        for i, w in enumerate(Y_CHUNKS):
-            add_h(3, c0, w)
-            quantise_h(3, c0, w)
-            y_product(HALF + c0, w, ((0, 1), (6, 7))[i % 2])
-            c0 = c0 + w
-        c0 = 0
-        for w in Y_CHUNKS:
-            y_round(HALF + c0, w)
-            y_quantise(HALF + c0, w)
-            c0 = c0 + w
+
+        for i in range(2):
+            last_piece_group0(i)
+        for i in range(2):
+            add_h(4, i * LAST, LAST)
+        for i in range(2):
+            quantise_h(4, i * LAST, LAST)
+            last_piece_group1(i)
+        round_y(HALF, QUARTER, nc.vector.tensor_copy)
+        for j0 in (0, QUARTER, HALF):
+            quantise_y(j0, QUARTER)
+        store_words(0, HALF + QUARTER)
+        for i in range(2):
+            round_y(S - QUARTER + i * LAST, LAST, nc.vector.tensor_copy)
+        for i in range(2):
+            quantise_y(S - QUARTER + i * LAST, LAST)
+        store_words(S - QUARTER, QUARTER)
 
         for q in range(4):
-            nc.sync.dma_start(out_2[0, 4 * q : 4 * q + 4, :].bitcast(I32), y_sc[32 * q : 32 * q + 4, :].bitcast(I32))
+            (nc.sync, nc.scalar)[q % 2].dma_start(out_2[0, q:16:4, :].bitcast(I32), y_sc[q:P:32, :].bitcast(I32))

import math
from contextlib import ExitStack

import concourse.mybir as mybir

K, K2, H, N, T, S = 512, 1024, 1024, 512, 4096, 1024
FLOPS = 2 * S * (2 * K * H + K2 * H + H * N)

F32 = mybir.dt.float32
BF16 = mybir.dt.bfloat16
I32 = mybir.dt.int32
U32 = mybir.dt.uint32
U16 = mybir.dt.uint16
U8 = mybir.dt.uint8
FP8X4 = mybir.dt.float8_e4m3fn_x4
FP4X4 = mybir.dt.float4_e2m1fn_x4
ACT = mybir.ActivationFunctionType
ALU = mybir.AluOpType

P = 128
PACK = 4
PASS = P * PACK
BANK = 512
HALF = S // 2
QUARTER = S // 4
LAST = S // 8
RUN = 4

BLOCKS = ((0, 0, HALF), (0, HALF, HALF), (1, 0, HALF), (1, HALF, QUARTER), (1, HALF + QUARTER, QUARTER))
UNITS = [(b, t) for b, (g, j0, w) in enumerate(BLOCKS) for t in range(0, PACK, BANK // w)]

ROUNDED_ON_SCALAR = ("wx11", "wo0")
WX10_VECTOR_SHARE = 88
PAIRS = {"wx01": ("wx_g1", 0), "wx11": ("wx_g1", 1), "wo0": ("wo", 0), "wo1": ("wo", 1)}

PIECE_BF16 = PASS * PACK * 2
PIECE_F32 = PASS * PACK * 4
TABLE_AT = PIECE_BF16
RAW_AT = [TABLE_AT + 4 * T + i * PIECE_F32 for i in range(4)]
SHARED = {
    "round_wx00": 0,
    "round_wx10": 0,
    "v_scales0": 0,
    "v_scales1": HALF,
    "wb_dealt": S,
    "wb_scales_dealt": S + 2 * H,
    "tab_w": TABLE_AT,
    "round_wa0": TABLE_AT,
    "round_wx_g1": TABLE_AT + PIECE_BF16,
    "round_wo": TABLE_AT,
    "wx00": RAW_AT[0],
    "tanh2": RAW_AT[0],
    "wx01": RAW_AT[0],
    "wx10": RAW_AT[1],
    "tanh1": RAW_AT[1],
    "wa0": RAW_AT[1],
    "wo0": RAW_AT[1],
    "tanh3": RAW_AT[2],
    "wx11": RAW_AT[2],
    "wo1": RAW_AT[2],
    "tanh4": RAW_AT[3],
    "wa1": RAW_AT[3],
}

OUT_BANKS = (6, 7)
LAST_BANKS = (4, 5)


def hand_bank(u):
    return u % 4 if u < 6 else 4 + u % 2


def motion_bank(u):
    if u < 4:
        return 4 + u
    return (0, 2, 6)[(u - 4) % 3] if u < 10 else 2 * (u % 2)


def shape_bank(u):
    return (2, 3, 6, 7)[u] if u < 4 else motion_bank(u) + 1


def tile_list_sign_caption_ranker_kernel(
    tc, tab_words, tab_scales, offs, xs_words, xs_scales, wa, wb_words, wb_scales, wx, span, wo, out_0, out_1, out_2
):
    nc = tc.nc
    with ExitStack() as ctx:
        keep = ctx.enter_context(tc.tile_pool(name="keep", bufs=1))
        ring = ctx.enter_context(tc.tile_pool(name="ring", bufs=3))
        reuse = ctx.enter_context(tc.tile_pool(name="reuse", bufs=1))
        psum = ctx.enter_context(tc.psum_pool(name="psum", bufs=1))

        def place(shape, dtype, name):
            if name in SHARED:
                return reuse.tile(shape, dtype, name=name, align_bytes=64, offset=SHARED[name])
            return keep.tile(shape, dtype, name=name, align_bytes=64)

        def bank_tile(number, slices, width):
            return psum.tile([P, slices, width], F32, name="bank", tag=f"bank{number}")

        def mx(out, lhs, lhs_scale, rhs, rhs_scale, start, stop, lhs_dtype=FP8X4):
            nc.tensor.matmul_mx(
                out,
                lhsT=lhs.bitcast(lhs_dtype),
                lhsT_scale=lhs_scale,
                rhs=rhs.bitcast(FP8X4),
                rhs_scale=rhs_scale,
                start=start,
                stop=stop,
            )

        def interleaved(tile):
            return tile.rearrange("p (c i t) -> p c t i", i=RUN, t=PACK)

        def by_slices(view):
            return view.rearrange("p t (c i) -> p c t i", i=RUN)

        offsets = keep.tile([P, S // 16], U16, name="offsets")
        xs_sc = place([P, S], U8, "xs_sc")
        tab_sc = place([P, T], U8, "tab_sc")
        wb_sc = place([P, H], U8, "wb_sc")
        tab_w = place([P, T], I32, "tab_w")
        wb_w = place([P, 2 * H], U8, "wb_w")
        span_t = keep.tile([P, 2, PACK], F32, name="span_t")
        minus_span = keep.tile([P, 2, PACK], F32, name="minus_span")
        zero = keep.tile([P, 1], F32, name="zero")
        tanh_bias = keep.tile([P, 1], F32, name="tanh_bias")
        one = keep.tile([P, 1], F32, name="one")
        half_pi = keep.tile([P, 1], F32, name="half_pi")

        nc.vector.memset(zero[:], 0.0)
        nc.scalar.activation(tanh_bias[:], zero[:], ACT.Silu)
        nc.vector.memset(xs_sc[:].bitcast(I32), 0)
        nc.vector.memset(tab_sc[:].bitcast(I32), 0)
        nc.vector.memset(wb_sc[:].bitcast(I32), 0)
        nc.vector.memset(one[:], 1.0)
        nc.vector.tensor_scalar(half_pi[:], one[:], math.pi / 2, None, ALU.mult)

        loaded = {}
        xs_w = {}

        def load_piece(name, weight, row0, col0):
            loaded[name] = place([P, PACK, PASS], F32, name)
            rows = weight[row0 : row0 + PASS, col0 : col0 + PASS]
            nc.sync.dma_start(loaded[name][:], rows.rearrange("(p j) c -> p j c", j=PACK))

        def load_xs(half):
            xs_w[half] = place([P, 2, HALF], I32, f"xs_w{half}")
            words = xs_words[:, :, half * HALF : (half + 1) * HALF, :].rearrange("a p c i -> p a (c i)")
            nc.sync.dma_start(xs_w[half][:], words.bitcast(I32))

        def load_scale_rows(tile, scales):
            for q in range(4):
                nc.sync.dma_start(tile[q:P:32, :].bitcast(I32), scales[0, q:16:4, :].bitcast(I32))

        load_piece("wx00", wx, 0, 0)
        load_piece("wx10", wx, PASS, 0)
        for quad in range(4):
            nc.sync.dma_start(
                xs_sc[32 * quad : 32 * quad + 8, :].bitcast(I32), xs_scales[:, 4 * quad : 4 * quad + 4, :].bitcast(I32)
            )
        load_xs(0)
        nc.sync.dma_start(span_t[:], span.rearrange("(g p t) -> p g t", g=2, t=PACK))
        nc.sync.dma_start(offsets[:], offs)
        load_scale_rows(tab_sc, tab_scales)
        nc.sync.dma_start(wb_w[:].bitcast(I32), wb_words[0].bitcast(I32))
        load_scale_rows(wb_sc, wb_scales)
        nc.sync.dma_start(tab_w[:], tab_words[0].rearrange("p n i -> p (n i)").bitcast(I32))
        load_xs(1)

        nc.gpsimd.tensor_scalar(minus_span[:], span_t[:], -1.0, 0.0, ALU.mult, ALU.add)

        rounded = {}
        weight_q = {}

        def round_piece(name):
            if name in PAIRS:
                pair, i = PAIRS[name]
                if i == 0:
                    rounded[pair] = place([P, 2 * PACK * PASS], BF16, "round_" + pair)
                target = rounded[pair][:, i * PACK * PASS : (i + 1) * PACK * PASS]
            else:
                rounded[name] = place([P, PACK * PASS], BF16, "round_" + name)
                target = rounded[name][:]
            dst = target.rearrange("p (t m j) -> p m j t", t=PACK, j=PACK)
            src = loaded[name][:].rearrange("p j (m t) -> p m j t", t=PACK)
            if name == "wx10":
                nc.vector.tensor_copy(dst[:, :WX10_VECTOR_SHARE], src[:, :WX10_VECTOR_SHARE])
                nc.scalar.copy(dst[:, WX10_VECTOR_SHARE:], src[:, WX10_VECTOR_SHARE:])
            elif name in ROUNDED_ON_SCALAR:
                nc.scalar.copy(dst, src)
            else:
                nc.vector.tensor_copy(dst, src)

        def quantise_weight(name, pieces):
            codes = place([P, len(pieces) * PASS], U32, "codes_" + name)
            scales = place([P, len(pieces) * PASS], U8, "scales_" + name)
            nc.vector.quantize_mx(codes[:].bitcast(FP8X4), scales[:], rounded[name][:])
            for i, piece in enumerate(pieces):
                weight_q[piece] = (codes[:, i * PASS : (i + 1) * PASS], scales[:, i * PASS : (i + 1) * PASS])

        wb_dealt = place([P, 2 * H], U8, "wb_dealt")
        wb_scales_dealt = place([P, H], U8, "wb_scales_dealt")

        def deal_wb():
            nc.vector.tensor_copy(
                wb_dealt[:].rearrange("p (g t m b) -> p g m t b", g=2, t=PACK, b=2),
                wb_w[:].rearrange("p (g m t b) -> p g m t b", g=2, t=PACK, b=2),
            )
            nc.vector.tensor_copy(
                wb_scales_dealt[:].rearrange("p (g t m) -> p g m t", g=2, t=PACK),
                wb_sc[:].rearrange("p (g m t) -> p g m t", g=2, t=PACK),
            )

        v_words = [place([P, HALF], U32, f"v_words{half}") for half in range(2)]
        v_scales = [place([P, HALF], U8, f"v_scales{half}") for half in range(2)]

        def gather(targets, window):
            for half in range(2):
                entries = offsets[:, half * HALF // 16 : (half + 1) * HALF // 16]
                nc.vector.tensor_copy(targets[half][:], window.indirect(entries))

        cos_t = {}
        sin_t = {}
        tanh_t = {}
        abs_t = {}

        def unit(u):
            b, t0 = UNITS[u]
            g, j0, w = BLOCKS[b]
            return b, g, j0, w, range(t0, t0 + BANK // w)

        def cosine(u):
            b, g, j0, w, slices = unit(u)
            for i, t in enumerate(slices):
                nc.scalar.activation(
                    cos_t[b][:, t, :], abs_t[u][:, i, :], ACT.Sin, scale=minus_span[:, g, t : t + 1], bias=half_pi[:]
                )

        def angles(u):
            b, g, j0, w, slices = unit(u)
            if slices[0] == 0:
                cos_t[b] = ring.tile([P, PACK, w], F32, name=f"cos{b}", tag="cos", bufs=4)
                sin_t[b] = ring.tile([P, PACK, w], F32, name=f"sin{b}", tag="sin", bufs=4)
            hand = bank_tile(hand_bank(u), len(slices), w)
            half, c0 = divmod(j0, HALF)
            for i, t in enumerate(slices):
                for a in (1, 0):
                    codes, scales = weight_q[f"wx{a}{g}"]
                    mx(
                        hand[:, i, :],
                        codes[:, t * P : (t + 1) * P],
                        scales[:, t * P : (t + 1) * P],
                        xs_w[half][:, a, c0 : c0 + w],
                        xs_sc[4 * a : P, j0 : j0 + w],
                        start=(a == 1),
                        stop=(a == 0),
                    )
            if f"tanh{u}" in SHARED:
                tanh_t[u] = place([P, len(slices), w], F32, f"tanh{u}")
            else:
                tanh_t[u] = ring.tile([P, len(slices), w], F32, name=f"tanh{u}", tag="tanh")
            nc.scalar.activation(tanh_t[u][:], hand[:], ACT.Tanh, bias=tanh_bias[:])
            if u >= 1:
                cosine(u - 1)
            abs_t[u] = ring.tile([P, len(slices), w], F32, name=f"abs{u}", tag="abs")
            nc.scalar.activation(abs_t[u][:], tanh_t[u][:], ACT.Abs)
            for i, t in enumerate(slices):
                nc.scalar.activation(sin_t[b][:, t, :], tanh_t[u][:, i, :], ACT.Sin, scale=span_t[:, g, t : t + 1])

        def motion_times_sine(u):
            b, g, j0, w, slices = unit(u)
            half, c0 = divmod(j0, HALF)
            motion = bank_tile(motion_bank(u), len(slices), w)
            for i, t in enumerate(slices):
                col = g * PASS + t * P
                mx(
                    motion[:, i, :],
                    wb_dealt[:, 2 * col : 2 * (col + P)],
                    wb_scales_dealt[:, col : col + P],
                    v_words[half][:, c0 : c0 + w],
                    v_scales[half][:, c0 : c0 + w],
                    start=True,
                    stop=True,
                    lhs_dtype=FP4X4,
                )
            rows = sin_t[b][:, slices[0] : slices[-1] + 1, :]
            nc.vector.tensor_tensor(rows, motion[:], rows, ALU.mult)

        def shape_times_cosine(u):
            b, g, j0, w, slices = unit(u)
            half, c0 = divmod(j0, HALF)
            shape = bank_tile(shape_bank(u), len(slices), w)
            codes, scales = weight_q[f"wa{g}"]
            for i, t in enumerate(slices):
                mx(
                    shape[:, i, :],
                    codes[:, t * P : (t + 1) * P],
                    scales[:, t * P : (t + 1) * P],
                    v_words[half][:, c0 : c0 + w],
                    v_scales[half][:, c0 : c0 + w],
                    start=True,
                    stop=True,
                )
            rows = cos_t[b][:, slices[0] : slices[-1] + 1, :]
            nc.vector.tensor_tensor(rows, shape[:], rows, ALU.mult)

        def products(u):
            motion_times_sine(u)
            shape_times_cosine(u)

        h_rounded = {}
        h_q = {}

        def add_h(b, c0, w):
            tag, bufs = ("h_wide", 1) if w == HALF else ("h_narrow", 3)
            h_rounded[b, c0] = ring.tile([P, PACK * w], BF16, name=f"hb{b}_{c0}", tag=tag, bufs=bufs, align_bytes=64)
            nc.vector.tensor_tensor(
                interleaved(h_rounded[b, c0][:]),
                by_slices(cos_t[b][:, :, c0 : c0 + w]),
                by_slices(sin_t[b][:, :, c0 : c0 + w]),
                ALU.add,
            )

        def quantise_h(b, c0, w):
            codes = place([P, w], U32, f"h_codes{b}_{c0}")
            scales = place([P, w], U8, f"h_scales{b}_{c0}")
            nc.vector.quantize_mx(codes[:].bitcast(FP8X4), scales[:], h_rounded[b, c0][:])
            h_q[b, c0] = (codes, scales)

        out_rows = out_0.rearrange("(p t) j -> p t j", t=PACK)
        out_words = out_1[0].rearrange("p m t -> p (m t)").bitcast(I32)
        y_words = place([P, S], I32, "y_words")
        y_sc = place([P, S], U8, "y_sc")
        y_f32 = {}
        y_rounded = {}
        last_sums = {}

        def out_pass(out, t, g, j0, w, b1, start, stop):
            if g == 0:
                half, c0 = divmod(j0, HALF)
                codes, scales = h_q[half, 0]
                codes, scales = codes[:, c0 : c0 + w], scales[:, c0 : c0 + w]
            else:
                codes, scales = h_q[b1, j0 - BLOCKS[b1][1]]
                codes, scales = codes[:], scales[:]
            wo_codes, wo_scales = weight_q[f"wo{g}"]
            mx(out, wo_codes[:, t * P : (t + 1) * P], wo_scales[:, t * P : (t + 1) * P], codes, scales, start, stop)

        def out_block(b1):
            j0, w = BLOCKS[b1][1:]
            y_f32[j0] = place([P, PACK, w], F32, f"y{j0}")
            per_bank = BANK // w
            for t0 in range(0, PACK, per_bank):
                sums = bank_tile(OUT_BANKS[(t0 // per_bank) % 2], per_bank, w)
                for i in range(per_bank):
                    for g in range(2):
                        out_pass(sums[:, i, :], t0 + i, g, j0, w, b1, start=(g == 0), stop=(g == 1))
                nc.scalar.copy(y_f32[j0][:, t0 : t0 + per_bank, :], sums[:])
                done = t0 + per_bank
                if done % 2 == 0:
                    nc.sync.dma_start(out_rows[:, done - 2 : done, j0 : j0 + w], y_f32[j0][:, done - 2 : done, :])

        def last_piece_group0(i):
            j0 = S - QUARTER + i * LAST
            last_sums[i] = bank_tile(LAST_BANKS[i], PACK, LAST)
            for t in range(PACK):
                out_pass(last_sums[i][:, t, :], t, 0, j0, LAST, 4, start=(t == 0), stop=False)

        def last_piece_group1(i):
            j0 = S - QUARTER + i * LAST
            for t in range(PACK):
                out_pass(last_sums[i][:, t, :], t, 1, j0, LAST, 4, start=False, stop=(t == PACK - 1))
            y_f32[j0] = place([P, PACK, LAST], F32, f"y{j0}")
            nc.scalar.copy(y_f32[j0][:], last_sums[i][:])
            nc.sync.dma_start(out_rows[:, :, j0 : j0 + LAST], y_f32[j0][:])

        def round_y(j0, w, copy):
            source = y_f32[0][:, :, j0 : j0 + w] if j0 < HALF else y_f32[j0][:]
            y_rounded[j0] = ring.tile([P, PACK * w], BF16, name=f"yb{j0}", tag="y_rounded", bufs=5, align_bytes=64)
            copy(interleaved(y_rounded[j0][:]), by_slices(source))

        def quantise_y(j0, w):
            nc.vector.quantize_mx(y_words[:, j0 : j0 + w].bitcast(FP8X4), y_sc[:, j0 : j0 + w], y_rounded[j0][:])

        def store_words(j0, w):
            nc.sync.dma_start(out_words[:, j0 : j0 + w], y_words[:, j0 : j0 + w])

        round_piece("wx00")
        quantise_weight("wx00", ["wx00"])
        round_piece("wx10")
        quantise_weight("wx10", ["wx10"])
        gather(v_scales, tab_sc[:])
        angles(0)
        angles(1)
        load_piece("wa0", wa, 0, 0)
        deal_wb()
        angles(2)
        load_piece("wx01", wx, 0, PASS)
        angles(3)
        load_piece("wx11", wx, PASS, PASS)
        gather(v_words, tab_w[:].bitcast(U32))
        angles(4)
        load_piece("wa1", wa, 0, PASS)

        for u in range(4):
            motion_times_sine(u)
        round_piece("wa0")
        load_piece("wo0", wo, 0, 0)
        motion_times_sine(4)
        quantise_weight("wa0", ["wa0"])
        angles(5)
        round_piece("wx01")
        shape_times_cosine(0)
        shape_times_cosine(1)
        angles(6)
        shape_times_cosine(2)
        shape_times_cosine(3)
        round_piece("wx11")
        load_piece("wo1", wo, PASS, 0)
        angles(7)
        shape_times_cosine(4)
        quantise_weight("wx_g1", ["wx01", "wx11"])
        add_h(0, 0, HALF)

        angles(8)
        motion_times_sine(5)
        quantise_h(0, 0, HALF)
        round_piece("wa1")
        shape_times_cosine(5)
        quantise_weight("wa1", ["wa1"])
        angles(9)
        products(6)
        round_piece("wo0")
        products(7)
        angles(10)
        products(8)
        round_piece("wo1")
        angles(11)
        products(9)
        quantise_weight("wo", ["wo0", "wo1"])
        angles(12)
        products(10)
        products(11)

        add_h(2, 0, HALF)
        angles(13)
        motion_times_sine(12)
        quantise_h(2, 0, HALF)
        out_block(2)
        shape_times_cosine(12)
        add_h(1, 0, HALF)
        angles(14)
        motion_times_sine(13)
        quantise_h(1, 0, HALF)
        angles(15)
        cosine(15)
        shape_times_cosine(13)
        add_h(3, 0, QUARTER)
        motion_times_sine(14)
        quantise_h(3, 0, QUARTER)
        out_block(3)
        round_y(0, QUARTER, nc.scalar.copy)
        round_y(QUARTER, QUARTER, nc.scalar.copy)
        shape_times_cosine(14)
        products(15)

        for i in range(2):
            last_piece_group0(i)
        for i in range(2):
            add_h(4, i * LAST, LAST)
        for i in range(2):
            quantise_h(4, i * LAST, LAST)
            last_piece_group1(i)
        round_y(HALF, QUARTER, nc.vector.tensor_copy)
        for j0 in (0, QUARTER, HALF):
            quantise_y(j0, QUARTER)
        store_words(0, HALF + QUARTER)
        for i in range(2):
            round_y(S - QUARTER + i * LAST, LAST, nc.vector.tensor_copy)
        for i in range(2):
            quantise_y(S - QUARTER + i * LAST, LAST)
        store_words(S - QUARTER, QUARTER)

        for q in range(4):
            (nc.sync, nc.scalar)[q % 2].dma_start(out_2[0, q:16:4, :].bitcast(I32), y_sc[q:P:32, :].bitcast(I32))
